import numpy as np
import ml_dtypes


def mxq(x, axis, fmt="e4m3"):
    dtype, down = {"e4m3": (ml_dtypes.float8_e4m3fn, 7), "e5m2": (ml_dtypes.float8_e5m2, 14)}[fmt]
    v = np.moveaxis(np.asarray(x, np.float32).astype(ml_dtypes.bfloat16).astype(np.float64), axis, -1)
    blocks = v.reshape(v.shape[:-1] + (-1, 32))
    amax = np.abs(blocks).max(-1, keepdims=True)
    byte = np.maximum(np.where(amax > 0, np.frexp(amax)[1] - 1 + 127, 0) - down, 1)
    scale = np.exp2(byte - 127.0)
    codes = (blocks / scale).astype(np.float32).astype(dtype).astype(np.float64)
    return np.moveaxis((codes * scale).reshape(v.shape), -1, axis)


WIDE = False


def mx_kscale(k):
    if not WIDE:
        return np.ones(k)
    levels = np.array([10, -10, 5, -5, 0])
    if k % 512:
        return np.exp2(np.random.permutation(np.resize(levels, k // 32))).repeat(32)
    a = np.empty((k // 512, 16))
    for p in range(k // 512):
        a[p, :8] = np.random.permutation(np.resize(levels, 8))
        for g in range(8):
            far = levels[np.abs(levels - a[p, g]) >= 10]
            a[p, g + 8] = far[np.random.randint(len(far))]
    return np.exp2(a.ravel()).repeat(32)


def f64(x):
    return np.asarray(x).astype(np.float64)


def striped(idx):
    return np.tile(np.asarray(idx).reshape(-1, 16).T, (8, 1)).astype(np.uint16)


def unstriped(offs):
    return offs[:16].T.reshape(-1).astype(np.int64)


def bf(x):
    return np.asarray(x, np.float32).astype(ml_dtypes.bfloat16)


def planes(Y):
    r, m = Y.shape
    b = f64(bf(Y)).reshape(r // 32, 32, m)
    amax = np.abs(b).max(1)
    byte = np.clip(np.where(amax > 0, np.frexp(amax)[1] - 1 + 127 - 7, 1), 1, 254)
    codes = (b * np.exp2(127.0 - byte)[:, None, :]).reshape(r, m).astype(np.float32).astype(ml_dtypes.float8_e4m3fn).view(np.uint8)
    words = codes.reshape(r // 512, 128, 4, m).transpose(0, 1, 3, 2)
    return np.ascontiguousarray(words), np.ascontiguousarray(byte.astype(np.uint8).reshape(r // 512, 16, m))


K, U, I, F = 512, 1024, 1024, 512


def setup_inputs():
    n = np.random.standard_normal
    idx = np.random.randint(0, U, I)
    idx2 = np.random.randint(0, U, I)
    idx3 = np.random.randint(0, U, I)
    fk = mx_kscale(K)
    return {
        "pa": (n((K, U)) / fk[:, None]).astype(np.float32),
        "pb": (n((K, U))).astype(np.float32),
        "pc_": (n((K, U))).astype(np.float32),
        "wo": (n((K, F)) * 1 / np.sqrt(K) * fk[:, None]).astype(np.float32),
        "bias": (0.3 * n((F, 1))).astype(np.float32),
        "offs": striped(idx),
        "offs2": striped(idx2),
        "offs3": striped(idx3),
    }


def reference(pa, pb, pc_, wo, bias, offs, offs2, offs3):
    idx = unstriped(offs)
    idx2 = unstriped(offs2)
    idx3 = unstriped(offs3)
    x = f64(pa)[:, idx] * f64(pb)[:, idx2] * f64(pc_)[:, idx3]
    woq = mxq(f64(wo), 0, "e4m3")
    xq = mxq(x, 0, "e4m3")
    z = woq.T @ xq
    y = np.maximum(z + f64(bias), 0.0)
    words, scales = planes(y)
    return y, words, scales

@@ -1,0 +1,189 @@
+from contextlib import ExitStack
+
+import concourse.mybir as mybir
+
+K, U, I, F = 512, 1024, 1024, 512
+FLOPS = 2 * K * F * I
+
+F32 = mybir.dt.float32
+BF16 = mybir.dt.bfloat16
+I32 = mybir.dt.int32
+U32 = mybir.dt.uint32
+U16 = mybir.dt.uint16
+U8 = mybir.dt.uint8
+FP8X4 = mybir.dt.float8_e4m3fn_x4
+MULT = mybir.AluOpType.mult
+ADD = mybir.AluOpType.add
+MAX = mybir.AluOpType.max
+COPY = mybir.ActivationFunctionType.Copy
+RELU = mybir.ActivationFunctionType.Relu
+
+P = 128
+PACK = 4
+BANK = 512
+CHUNKS = (512, 256, 128, 128)
+HALF = CHUNKS[0]
+
+
+def tile_attend_planefeatures_pl_kernel(tc, pa, pb, pc_, wo, bias, offs, offs2, offs3, out_0, out_1, out_2):
+    nc = tc.nc
+    starts = [sum(CHUNKS[:j]) for j in range(len(CHUNKS))]
+    last = len(CHUNKS) - 1
+
+    with ExitStack() as ctx:
+        keep = ctx.enter_context(tc.tile_pool(name="keep", bufs=1))
+        psum = ctx.enter_context(tc.psum_pool(name="psum", bufs=8))
+
+        lists = {}
+        tables = {}
+        sources = {"a": (pa, offs), "b": (pb, offs2), "c": (pc_, offs3)}
+        for pair in range(2):
+            for name in "abc":
+                table, offsets = sources[name]
+                if pair == 0:
+                    lists[name] = keep.tile([P, I // 16], U16, name="list_" + name)
+                    nc.sync.dma_start(lists[name][:], offsets)
+                for t in (2 * pair, 2 * pair + 1):
+                    tables[name, t] = keep.tile([P, U], F32, name="table_%s%d" % (name, t))
+                    nc.sync.dma_start(tables[name, t][:], table.rearrange("(p t) u -> p t u", t=PACK)[:, t, :])
+        w_raw = keep.tile([P, PACK * F], F32)
+        nc.sync.dma_start(w_raw[:], wo.rearrange("(p j) f -> p (j f)", j=PACK))
+        bias_sb = keep.tile([P, PACK], F32)
+        nc.sync.dma_start(bias_sb[:], bias.rearrange("(p t) o -> p (t o)", t=PACK))
+
+        work_u = keep.tile([P, 2 * HALF], F32)
+        work_v = keep.tile([P, 2 * HALF], F32)
+        work = [work_u, work_v, work_u, work_v, w_raw, work_u, work_v, work_u, work_v]
+        x = keep.tile([P, PACK, HALF], F32)
+        y_codes = keep.tile([P, I], U32, align_bytes=64)
+        y_scales = keep.tile([P, I], U8, align_bytes=64)
+        out_rows = out_0.rearrange("(p t) i -> p t i", t=PACK)
+        out_words = out_1[0].rearrange("p c r -> p (c r)").bitcast(I32)
+        out_scales = out_2[0].bitcast(I32)
+
+        def looked_up(name, t, j):
+            return tables[name, t][:].indirect(lists[name][:, starts[j] // 16 : (starts[j] + CHUNKS[j]) // 16])
+
+        def first_place(j, t):
+            unit, n = 2 * j + t // 2, CHUNKS[j]
+            begin = HALF - n // 2 + (t % 2) * n if unit == 2 else (t % 2) * HALF
+            return work[unit][:, begin : begin + n]
+
+        def second_place(j, t):
+            unit, n = 2 * j + t // 2, CHUNKS[j]
+            begin = (t % 2) * HALF
+            return work[unit + 1][:, begin : begin + n]
+
+        def gather_a(j, pair):
+            for t in (2 * pair, 2 * pair + 1):
+                nc.vector.tensor_copy(first_place(j, t), looked_up("a", t, j))
+
+        def gather_b(j, pair):
+            for t in (2 * pair, 2 * pair + 1):
+                nc.vector.tensor_tensor(second_place(j, t), looked_up("b", t, j), first_place(j, t), MULT)
+
+        def gather_c(j, pair):
+            for t in (2 * pair, 2 * pair + 1):
+                nc.vector.tensor_tensor(x[:, t, : CHUNKS[j]], looked_up("c", t, j), second_place(j, t), MULT)
+
+        def interleave(grouped, planes, on_vector):
+            dst = grouped[:].rearrange("p (c i t) -> p c t i", i=4, t=PACK)
+            src = planes.rearrange("p t (c i) -> p c t i", i=4)
+            if on_vector:
+                nc.vector.tensor_copy(dst, src)
+            else:
+                nc.scalar.activation(dst, src, COPY)
+
+        x_grouped, x_codes, x_scales, y, y_grouped, banks = {}, {}, {}, {}, {}, {}
+
+        def round_x(j):
+            n = CHUNKS[j]
+            x_grouped[j] = keep.tile([P, PACK * n], BF16, name="x_grouped%d" % j, tag="swap%d" % ((j + 1) % 2), align_bytes=64)
+            interleave(x_grouped[j], x[:, :, :n], j == last)
+
+        def quantize_x(j):
+            n = CHUNKS[j]
+            x_codes[j] = keep.tile([P, n], U32, name="x_codes%d" % j, tag="swap%d" % (j % 2), align_bytes=64)
+            x_scales[j] = keep.tile([P, n], U8, name="x_scales%d" % j, align_bytes=64)
+            nc.vector.quantize_mx(out=x_codes[j][:].bitcast(FP8X4), scales=x_scales[j][:], in_=x_grouped[j][:])
+
+        def multiply(j):
+            n = CHUNKS[j]
+            per_bank = 2 if j == last else BANK // n
+            for t in range(PACK):
+                if t % per_bank == 0:
+                    bank = psum.tile([P, per_bank, n], F32, name="bank")
+                banks[j, t] = bank[:, t % per_bank, :]
+                nc.tensor.matmul_mx(
+                    out=banks[j, t],
+                    lhsT=w_codes[:, t * P : (t + 1) * P].bitcast(FP8X4),
+                    lhsT_scale=w_scales[:, t * P : (t + 1) * P],
+                    rhs=x_codes[j][:].bitcast(FP8X4),
+                    rhs_scale=x_scales[j][:],
+                    start=True,
+                    stop=True,
+                )
+
+        def finish(j):
+            n = CHUNKS[j]
+            y[j] = keep.tile([P, PACK, n], F32, name="y%d" % j)
+            for t in range(PACK):
+                if j == last and t >= 2:
+                    nc.vector.tensor_scalar(y[j][:, t, :], banks[j, t], bias_sb[:, t : t + 1], 0.0, ADD, MAX)
+                else:
+                    nc.scalar.activation(y[j][:, t, :], banks[j, t], RELU, bias=bias_sb[:, t : t + 1])
+            nc.sync.dma_start(out_rows[:, :, starts[j] : starts[j] + n], y[j][:])
+
+        def round_y(j):
+            y_grouped[j] = keep.tile([P, PACK * CHUNKS[j]], BF16, name="y_grouped%d" % j, align_bytes=64)
+            interleave(y_grouped[j], y[j][:], j == last)
+
+        def quantize_y(j):
+            cols = slice(starts[j], starts[j] + CHUNKS[j])
+            nc.vector.quantize_mx(out=y_codes[:, cols].bitcast(FP8X4), scales=y_scales[:, cols], in_=y_grouped[j][:])
+            nc.sync.dma_start(out_words[:, cols], y_codes[:, cols].bitcast(I32))
+
+        w_grouped = keep.tile([P, PACK * F], BF16, align_bytes=64)
+        w_codes = keep.tile([P, F], U32, align_bytes=64)
+        w_scales = keep.tile([P, F], U8, align_bytes=64)
+
+        for pair in range(2):
+            gather_a(0, pair)
+            gather_b(0, pair)
+            gather_c(0, pair)
+        round_x(0)
+        nc.scalar.activation(
+            w_grouped[:].rearrange("p (t m j) -> p m j t", t=PACK, j=PACK),
+            w_raw[:].rearrange("p (j m t) -> p m j t", t=PACK, j=PACK),
+            COPY,
+        )
+        for j in range(1, len(CHUNKS)):
+            gather_a(j, 0)
+            gather_b(j, 0)
+            quantize_x(j - 1)
+            if j > 1:
+                multiply(j - 1)
+                finish(j - 1)
+            gather_c(j, 0)
+            gather_a(j, 1)
+            if j == 1:
+                nc.vector.quantize_mx(out=w_codes[:].bitcast(FP8X4), scales=w_scales[:], in_=w_grouped[:])
+                multiply(0)
+                finish(0)
+            gather_b(j, 1)
+            gather_c(j, 1)
+            if j > 1:
+                quantize_y(j - 2)
+            if j < last:
+                round_x(j)
+            round_y(j - 1)
+        round_x(last)
+        quantize_x(last)
+        multiply(last)
+        quantize_y(last - 1)
+        finish(last)
+        round_y(last)
+        quantize_y(last)
+        for q in range(4):
+            queue = nc.sync if q % 2 == 0 else nc.scalar
+            queue.dma_start(out_scales[4 * q : 4 * q + 4, :], y_scales[32 * q : 32 * q + 4, :].bitcast(I32))

@@ -21,18 +21,21 @@ RELU = mybir.ActivationFunctionType.Relu
 P = 128
 PACK = 4
 BANK = 512
-CHUNKS = (512, 256, 128, 128)
-HALF = CHUNKS[0]
+HALF = 512
+STRETCHES = ((0, 256), (256, 256), (512, 256), (768, 128), (896, 128))
 
 
 def tile_attend_planefeatures_pl_kernel(tc, pa, pb, pc_, wo, bias, offs, offs2, offs3, out_0, out_1, out_2):
     nc = tc.nc
-    starts = [sum(CHUNKS[:j]) for j in range(len(CHUNKS))]
-    last = len(CHUNKS) - 1
+    last = len(STRETCHES) - 1
 
     with ExitStack() as ctx:
         keep = ctx.enter_context(tc.tile_pool(name="keep", bufs=1))
+        laid = ctx.enter_context(tc.tile_pool(name="laid", bufs=1))
         psum = ctx.enter_context(tc.psum_pool(name="psum", bufs=8))
+
+        def placed(name, shape, dtype, offset):
+            return laid.tile(shape, dtype, name=name, offset=offset, align_bytes=64)
 
         lists = {}
         tables = {}
@@ -40,51 +43,38 @@ def tile_attend_planefeatures_pl_kernel(tc, pa, pb, pc_, wo, bias, offs, offs2, 
         for pair in range(2):
             for name in "abc":
                 table, offsets = sources[name]
-                if pair == 0:
-                    lists[name] = keep.tile([P, I // 16], U16, name="list_" + name)
-                    nc.sync.dma_start(lists[name][:], offsets)
                 for t in (2 * pair, 2 * pair + 1):
                     tables[name, t] = keep.tile([P, U], F32, name="table_%s%d" % (name, t))
                     nc.sync.dma_start(tables[name, t][:], table.rearrange("(p t) u -> p t u", t=PACK)[:, t, :])
-        w_raw = keep.tile([P, PACK * F], F32)
+                    if t == 0:
+                        lists[name] = keep.tile([P, I // 16], U16, name="list_" + name)
+                        nc.sync.dma_start(lists[name][:], offsets)
+        W_AT, X0_AT, X2_AT, X3_AT, LAST_AT = 0, 8192, 16384, 20480, 24576
+        w_raw = placed("w_raw", [P, PACK * F], F32, W_AT)
         nc.sync.dma_start(w_raw[:], wo.rearrange("(p j) f -> p (j f)", j=PACK))
         bias_sb = keep.tile([P, PACK], F32)
         nc.sync.dma_start(bias_sb[:], bias.rearrange("(p t) o -> p (t o)", t=PACK))
 
         work_u = keep.tile([P, 2 * HALF], F32)
         work_v = keep.tile([P, 2 * HALF], F32)
-        work = [work_u, work_v, work_u, work_v, w_raw, work_u, work_v, work_u, work_v]
-        x = keep.tile([P, PACK, HALF], F32)
-        y_codes = keep.tile([P, I], U32, align_bytes=64)
         y_scales = keep.tile([P, I], U8, align_bytes=64)
         out_rows = out_0.rearrange("(p t) i -> p t i", t=PACK)
         out_words = out_1[0].rearrange("p c r -> p (c r)").bitcast(I32)
         out_scales = out_2[0].bitcast(I32)
 
-        def looked_up(name, t, j):
-            return tables[name, t][:].indirect(lists[name][:, starts[j] // 16 : (starts[j] + CHUNKS[j]) // 16])
+        def looked_up(name, t, first, n):
+            return tables[name, t][:].indirect(lists[name][:, first // 16 : (first + n) // 16])
 
-        def first_place(j, t):
-            unit, n = 2 * j + t // 2, CHUNKS[j]
-            begin = HALF - n // 2 + (t % 2) * n if unit == 2 else (t % 2) * HALF
-            return work[unit][:, begin : begin + n]
+        def halves(work, n):
+            return [work[:, 0:n], work[:, HALF : HALF + n]]
 
-        def second_place(j, t):
-            unit, n = 2 * j + t // 2, CHUNKS[j]
-            begin = (t % 2) * HALF
-            return work[unit + 1][:, begin : begin + n]
+        def gather_a(pair, first, n, dst):
+            for h in range(2):
+                nc.vector.tensor_copy(dst[h], looked_up("a", 2 * pair + h, first, n))
 
-        def gather_a(j, pair):
-            for t in (2 * pair, 2 * pair + 1):
-                nc.vector.tensor_copy(first_place(j, t), looked_up("a", t, j))
-
-        def gather_b(j, pair):
-            for t in (2 * pair, 2 * pair + 1):
-                nc.vector.tensor_tensor(second_place(j, t), looked_up("b", t, j), first_place(j, t), MULT)
-
-        def gather_c(j, pair):
-            for t in (2 * pair, 2 * pair + 1):
-                nc.vector.tensor_tensor(x[:, t, : CHUNKS[j]], looked_up("c", t, j), second_place(j, t), MULT)
+        def gather_times(name, pair, first, n, dst, factor):
+            for h in range(2):
+                nc.vector.tensor_tensor(dst[h], looked_up(name, 2 * pair + h, first, n), factor[h], MULT)
 
         def interleave(grouped, planes, on_vector):
             dst = grouped[:].rearrange("p (c i t) -> p c t i", i=4, t=PACK)
@@ -96,20 +86,26 @@ def tile_attend_planefeatures_pl_kernel(tc, pa, pb, pc_, wo, bias, offs, offs2, 
 
         x_grouped, x_codes, x_scales, y, y_grouped, banks = {}, {}, {}, {}, {}, {}
 
-        def round_x(j):
-            n = CHUNKS[j]
-            x_grouped[j] = keep.tile([P, PACK * n], BF16, name="x_grouped%d" % j, tag="swap%d" % ((j + 1) % 2), align_bytes=64)
-            interleave(x_grouped[j], x[:, :, :n], j == last)
+        def round_x(j, planes, at=None):
+            n = STRETCHES[j][1]
+            if at is None:
+                x_grouped[j] = keep.tile([P, PACK * n], BF16, name="x_grouped%d" % j, align_bytes=64)
+            else:
+                x_grouped[j] = placed("x_grouped%d" % j, [P, PACK * n], BF16, at)
+            interleave(x_grouped[j], planes, j == last)
 
-        def quantize_x(j):
-            n = CHUNKS[j]
-            x_codes[j] = keep.tile([P, n], U32, name="x_codes%d" % j, tag="swap%d" % (j % 2), align_bytes=64)
+        def quantize_x(j, at=None):
+            n = STRETCHES[j][1]
+            if at is None:
+                x_codes[j] = keep.tile([P, n], U32, name="x_codes%d" % j, align_bytes=64)
+            else:
+                x_codes[j] = placed("x_codes%d" % j, [P, n], U32, at)
             x_scales[j] = keep.tile([P, n], U8, name="x_scales%d" % j, align_bytes=64)
             nc.vector.quantize_mx(out=x_codes[j][:].bitcast(FP8X4), scales=x_scales[j][:], in_=x_grouped[j][:])
 
         def multiply(j):
-            n = CHUNKS[j]
-            per_bank = 2 if j == last else BANK // n
+            n = STRETCHES[j][1]
+            per_bank = 1 if j == last else BANK // n
             for t in range(PACK):
                 if t % per_bank == 0:
                     bank = psum.tile([P, per_bank, n], F32, name="bank")
@@ -125,65 +121,113 @@ def tile_attend_planefeatures_pl_kernel(tc, pa, pb, pc_, wo, bias, offs, offs2, 
                 )
 
         def finish(j):
-            n = CHUNKS[j]
+            first, n = STRETCHES[j]
             y[j] = keep.tile([P, PACK, n], F32, name="y%d" % j)
             for t in range(PACK):
-                if j == last and t >= 2:
+                if j == last and t % 2 == 1:
                     nc.vector.tensor_scalar(y[j][:, t, :], banks[j, t], bias_sb[:, t : t + 1], 0.0, ADD, MAX)
                 else:
                     nc.scalar.activation(y[j][:, t, :], banks[j, t], RELU, bias=bias_sb[:, t : t + 1])
-            nc.sync.dma_start(out_rows[:, :, starts[j] : starts[j] + n], y[j][:])
+            nc.sync.dma_start(out_rows[:, :, first : first + n], y[j][:])
 
         def round_y(j):
-            y_grouped[j] = keep.tile([P, PACK * CHUNKS[j]], BF16, name="y_grouped%d" % j, align_bytes=64)
+            y_grouped[j] = keep.tile([P, PACK * STRETCHES[j][1]], BF16, name="y_grouped%d" % j, align_bytes=64)
             interleave(y_grouped[j], y[j][:], j == last)
 
-        def quantize_y(j):
-            cols = slice(starts[j], starts[j] + CHUNKS[j])
-            nc.vector.quantize_mx(out=y_codes[:, cols].bitcast(FP8X4), scales=y_scales[:, cols], in_=y_grouped[j][:])
-            nc.sync.dma_start(out_words[:, cols], y_codes[:, cols].bitcast(I32))
+        def quantize_y(j, at=None):
+            first, n = STRETCHES[j]
+            cols = slice(first, first + n)
+            if at is None:
+                y_codes = keep.tile([P, n], U32, name="y_codes%d" % j, align_bytes=64)
+            else:
+                y_codes = placed("y_codes%d" % j, [P, n], U32, at)
+            nc.vector.quantize_mx(out=y_codes[:].bitcast(FP8X4), scales=y_scales[:, cols], in_=y_grouped[j][:])
+            nc.sync.dma_start(out_words[:, cols], y_codes[:].bitcast(I32))
+
+        def pair_at(name, n, at):
+            return [placed("%s%d" % (name, h), [P, n], F32, at + 4 * n * h)[:] for h in range(2)]
 
         w_grouped = keep.tile([P, PACK * F], BF16, align_bytes=64)
         w_codes = keep.tile([P, F], U32, align_bytes=64)
         w_scales = keep.tile([P, F], U8, align_bytes=64)
 
-        for pair in range(2):
-            gather_a(0, pair)
-            gather_b(0, pair)
-            gather_c(0, pair)
-        round_x(0)
+        x0 = placed("x0", [P, PACK, 512], F32, X0_AT)
+        gather_a(0, 0, 512, halves(work_u, 512))
+        gather_times("b", 0, 0, 512, halves(work_v, 512), halves(work_u, 512))
+        gather_times("c", 0, 0, 512, [x0[:, 0, :], x0[:, 1, :]], halves(work_v, 512))
+        gather_a(1, 0, 512, halves(work_v, 512))
+        gather_times("b", 1, 0, 512, halves(work_u, 512), halves(work_v, 512))
+        nc.vector.tensor_tensor(x0[:, 2, :], looked_up("c", 2, 0, 512), work_u[:, 0:512], MULT)
+        for first in (0, 256):
+            nc.vector.tensor_tensor(
+                x0[:, 3, first : first + 256], looked_up("c", 3, first, 256), work_u[:, HALF + first : HALF + first + 256], MULT
+            )
+        round_x(0, x0[:, :, 0:256])
         nc.scalar.activation(
             w_grouped[:].rearrange("p (t m j) -> p m j t", t=PACK, j=PACK),
             w_raw[:].rearrange("p (j m t) -> p m j t", t=PACK, j=PACK),
             COPY,
         )
-        for j in range(1, len(CHUNKS)):
-            gather_a(j, 0)
-            gather_b(j, 0)
-            quantize_x(j - 1)
-            if j > 1:
-                multiply(j - 1)
-                finish(j - 1)
-            gather_c(j, 0)
-            gather_a(j, 1)
-            if j == 1:
-                nc.vector.quantize_mx(out=w_codes[:].bitcast(FP8X4), scales=w_scales[:], in_=w_grouped[:])
-                multiply(0)
-                finish(0)
-            gather_b(j, 1)
-            gather_c(j, 1)
-            if j > 1:
-                quantize_y(j - 2)
-            if j < last:
-                round_x(j)
-            round_y(j - 1)
-        round_x(last)
+        round_x(1, x0[:, :, 256:512], W_AT)
+
+        x2 = placed("x2", [P, PACK, 256], F32, X2_AT)
+        middle = [work_u[:, 384:640], work_u[:, 640:896]]
+        gather_a(0, 512, 256, middle)
+        gather_times("b", 0, 512, 256, halves(work_v, 256), middle)
+        gather_times("c", 0, 512, 256, [x2[:, 0, :], x2[:, 1, :]], halves(work_v, 256))
+        nc.vector.quantize_mx(out=w_codes[:].bitcast(FP8X4), scales=w_scales[:], in_=w_grouped[:])
+        quantize_x(0, W_AT + 4096)
+        multiply(0)
+        finish(0)
+        on_w = pair_at("on_w", 256, W_AT + 2048)
+        gather_a(1, 512, 256, on_w)
+        quantize_x(1)
+        multiply(1)
+        finish(1)
+        round_y(0)
+        on_x0 = pair_at("on_x0", 256, X0_AT)
+        gather_times("b", 1, 512, 256, on_x0, on_w)
+        gather_times("c", 1, 512, 256, [x2[:, 2, :], x2[:, 3, :]], on_x0)
+        round_x(2, x2[:])
+        round_y(1)
+
+        x3 = placed("x3", [P, PACK, 128], F32, X3_AT)
+        start = [on_x0[0][:, 0:128], on_x0[1][:, 0:128]]
+        gather_a(0, 768, 128, start)
+        gather_times("b", 0, 768, 128, halves(work_u, 128), start)
+        gather_times("c", 0, 768, 128, [x3[:, 0, :], x3[:, 1, :]], halves(work_u, 128))
+        quantize_x(2)
+        multiply(2)
+        finish(2)
+        on_x2 = pair_at("on_x2", 128, X2_AT)
+        gather_a(1, 768, 128, on_x2)
+        gather_times("b", 1, 768, 128, halves(work_v, 128), on_x2)
+        gather_times("c", 1, 768, 128, [x3[:, 2, :], x3[:, 3, :]], halves(work_v, 128))
+        round_x(3, x3[:])
+        round_y(2)
+
+        x4 = keep.tile([P, PACK, 128], F32)
+        gather_a(0, 896, 128, halves(work_v, 128))
+        gather_times("b", 0, 896, 128, halves(work_u, 128), halves(work_v, 128))
+        gather_times("c", 0, 896, 128, [x4[:, 0, :], x4[:, 1, :]], halves(work_u, 128))
+        quantize_x(3)
+        multiply(3)
+        finish(3)
+        round_y(3)
+        on_x3 = pair_at("on_x3", 128, X3_AT)
+        gather_a(1, 896, 128, on_x3)
+        gather_times("b", 1, 896, 128, halves(work_v, 128), on_x3)
+        gather_times("c", 1, 896, 128, [x4[:, 2, :], x4[:, 3, :]], halves(work_v, 128))
+        quantize_y(0)
+        round_x(last, x4[:], LAST_AT)
         quantize_x(last)
         multiply(last)
-        quantize_y(last - 1)
         finish(last)
         round_y(last)
         quantize_y(last)
+        quantize_y(1, LAST_AT - 768)
+        quantize_y(2, LAST_AT + 768)
+        quantize_y(3, LAST_AT + 256)
         for q in range(4):
             queue = nc.sync if q % 2 == 0 else nc.scalar
             queue.dma_start(out_scales[4 * q : 4 * q + 4, :], y_scales[32 * q : 32 * q + 4, :].bitcast(I32))

@@ -21,8 +21,8 @@ RELU = mybir.ActivationFunctionType.Relu
 P = 128
 PACK = 4
 BANK = 512
-HALF = 512
-STRETCHES = ((0, 256), (256, 256), (512, 256), (768, 128), (896, 128))
+HALF = 768
+STRETCHES = ((0, 256), (256, 256), (512, 256), (896, 128), (768, 128))
 
 
 def tile_attend_planefeatures_pl_kernel(tc, pa, pb, pc_, wo, bias, offs, offs2, offs3, out_0, out_1, out_2):
@@ -49,9 +49,10 @@ def tile_attend_planefeatures_pl_kernel(tc, pa, pb, pc_, wo, bias, offs, offs2, 
                     if t == 0:
                         lists[name] = keep.tile([P, I // 16], U16, name="list_" + name)
                         nc.sync.dma_start(lists[name][:], offsets)
-        W_AT, X0_AT, X2_AT, X3_AT, LAST_AT = 0, 8192, 16384, 20480, 24576
-        w_raw = placed("w_raw", [P, PACK * F], F32, W_AT)
-        nc.sync.dma_start(w_raw[:], wo.rearrange("(p j) f -> p (j f)", j=PACK))
+            if pair == 0:
+                w_raw = keep.tile([P, PACK * F], F32)
+                nc.sync.dma_start(w_raw[:], wo.rearrange("(p j) f -> p (j f)", j=PACK))
+        X_AT, CODES_AT, LAST_AT = 0, 12288, 16384
         bias_sb = keep.tile([P, PACK], F32)
         nc.sync.dma_start(bias_sb[:], bias.rearrange("(p t) o -> p (t o)", t=PACK))
 
@@ -92,7 +93,7 @@ def tile_attend_planefeatures_pl_kernel(tc, pa, pb, pc_, wo, bias, offs, offs2, 
                 x_grouped[j] = keep.tile([P, PACK * n], BF16, name="x_grouped%d" % j, align_bytes=64)
             else:
                 x_grouped[j] = placed("x_grouped%d" % j, [P, PACK * n], BF16, at)
-            interleave(x_grouped[j], planes, j == last)
+            interleave(x_grouped[j], planes, False)
 
         def quantize_x(j, at=None):
             n = STRETCHES[j][1]
@@ -144,82 +145,73 @@ def tile_attend_planefeatures_pl_kernel(tc, pa, pb, pc_, wo, bias, offs, offs2, 
             nc.vector.quantize_mx(out=y_codes[:].bitcast(FP8X4), scales=y_scales[:, cols], in_=y_grouped[j][:])
             nc.sync.dma_start(out_words[:, cols], y_codes[:].bitcast(I32))
 
-        def pair_at(name, n, at):
-            return [placed("%s%d" % (name, h), [P, n], F32, at + 4 * n * h)[:] for h in range(2)]
-
         w_grouped = keep.tile([P, PACK * F], BF16, align_bytes=64)
         w_codes = keep.tile([P, F], U32, align_bytes=64)
         w_scales = keep.tile([P, F], U8, align_bytes=64)
 
-        x0 = placed("x0", [P, PACK, 512], F32, X0_AT)
-        gather_a(0, 0, 512, halves(work_u, 512))
-        gather_times("b", 0, 0, 512, halves(work_v, 512), halves(work_u, 512))
-        gather_times("c", 0, 0, 512, [x0[:, 0, :], x0[:, 1, :]], halves(work_v, 512))
-        gather_a(1, 0, 512, halves(work_v, 512))
-        gather_times("b", 1, 0, 512, halves(work_u, 512), halves(work_v, 512))
-        nc.vector.tensor_tensor(x0[:, 2, :], looked_up("c", 2, 0, 512), work_u[:, 0:512], MULT)
-        for first in (0, 256):
-            nc.vector.tensor_tensor(
-                x0[:, 3, first : first + 256], looked_up("c", 3, first, 256), work_u[:, HALF + first : HALF + first + 256], MULT
-            )
-        round_x(0, x0[:, :, 0:256])
+        x = placed("x", [P, PACK, 768], F32, X_AT)
+        gather_a(0, 0, 768, halves(work_u, 768))
+        gather_times("b", 0, 0, 768, halves(work_v, 768), halves(work_u, 768))
+        gather_times("c", 0, 0, 768, [x[:, 0, :], x[:, 1, :]], halves(work_v, 768))
         nc.scalar.activation(
             w_grouped[:].rearrange("p (t m j) -> p m j t", t=PACK, j=PACK),
             w_raw[:].rearrange("p (j m t) -> p m j t", t=PACK, j=PACK),
             COPY,
         )
-        round_x(1, x0[:, :, 256:512], W_AT)
-
-        x2 = placed("x2", [P, PACK, 256], F32, X2_AT)
-        middle = [work_u[:, 384:640], work_u[:, 640:896]]
-        gather_a(0, 512, 256, middle)
-        gather_times("b", 0, 512, 256, halves(work_v, 256), middle)
-        gather_times("c", 0, 512, 256, [x2[:, 0, :], x2[:, 1, :]], halves(work_v, 256))
+        gather_a(1, 0, 512, halves(work_v, 512))
         nc.vector.quantize_mx(out=w_codes[:].bitcast(FP8X4), scales=w_scales[:], in_=w_grouped[:])
-        quantize_x(0, W_AT + 4096)
+        near = [work_u[:, 0:512], work_u[:, 512:1024]]
+        gather_times("b", 1, 0, 512, near, halves(work_v, 512))
+        nc.vector.tensor_tensor(x[:, 2, 0:512], looked_up("c", 2, 0, 512), near[0], MULT)
+        for first in (0, 256):
+            nc.vector.tensor_tensor(
+                x[:, 3, first : first + 256], looked_up("c", 3, first, 256), work_u[:, 512 + first : 768 + first], MULT
+            )
+        round_x(0, x[:, :, 0:256])
+        round_x(1, x[:, :, 256:512])
+
+        middle = [work_u[:, 384:640], work_u[:, 640:896]]
+        gather_a(1, 512, 256, middle)
+        quantize_x(0, CODES_AT)
         multiply(0)
         finish(0)
-        on_w = pair_at("on_w", 256, W_AT + 2048)
-        gather_a(1, 512, 256, on_w)
+        round_y(0)
+        freed = [x[:, 0, 0:256], x[:, 1, 0:256]]
+        gather_times("b", 1, 512, 256, freed, middle)
+        gather_times("c", 1, 512, 256, [x[:, 2, 512:768], x[:, 3, 512:768]], freed)
+        round_x(2, x[:, :, 512:768], CODES_AT)
         quantize_x(1)
         multiply(1)
         finish(1)
-        round_y(0)
-        on_x0 = pair_at("on_x0", 256, X0_AT)
-        gather_times("b", 1, 512, 256, on_x0, on_w)
-        gather_times("c", 1, 512, 256, [x2[:, 2, :], x2[:, 3, :]], on_x0)
-        round_x(2, x2[:])
         round_y(1)
 
-        x3 = placed("x3", [P, PACK, 128], F32, X3_AT)
-        start = [on_x0[0][:, 0:128], on_x0[1][:, 0:128]]
-        gather_a(0, 768, 128, start)
-        gather_times("b", 0, 768, 128, halves(work_u, 128), start)
-        gather_times("c", 0, 768, 128, [x3[:, 0, :], x3[:, 1, :]], halves(work_u, 128))
+        freed = [x[:, 0, 256:512], x[:, 1, 256:512]]
+        gather_a(0, 768, 256, freed)
+        gather_times("b", 0, 768, 256, halves(work_v, 256), freed)
         quantize_x(2)
         multiply(2)
         finish(2)
-        on_x2 = pair_at("on_x2", 128, X2_AT)
-        gather_a(1, 768, 128, on_x2)
-        gather_times("b", 1, 768, 128, halves(work_v, 128), on_x2)
-        gather_times("c", 1, 768, 128, [x3[:, 2, :], x3[:, 3, :]], halves(work_v, 128))
-        round_x(3, x3[:])
+        x_end = placed("x_end", [P, PACK, 256], F32, X_AT)
+        gather_times("c", 0, 768, 256, [x_end[:, 0, :], x_end[:, 1, :]], halves(work_v, 256))
         round_y(2)
+        gather_a(1, 896, 128, halves(work_v, 128))
+        gather_times("b", 1, 896, 128, halves(work_u, 128), halves(work_v, 128))
+        gather_times("c", 1, 896, 128, [x_end[:, 2, 128:256], x_end[:, 3, 128:256]], halves(work_u, 128))
+        round_x(3, x_end[:, :, 128:256])
 
-        x4 = keep.tile([P, PACK, 128], F32)
-        gather_a(0, 896, 128, halves(work_v, 128))
-        gather_times("b", 0, 896, 128, halves(work_u, 128), halves(work_v, 128))
-        gather_times("c", 0, 896, 128, [x4[:, 0, :], x4[:, 1, :]], halves(work_u, 128))
+        gather_a(1, 768, 128, halves(work_u, 128))
+        gather_times("b", 1, 768, 128, halves(work_v, 128), halves(work_u, 128))
         quantize_x(3)
         multiply(3)
         finish(3)
         round_y(3)
-        on_x3 = pair_at("on_x3", 128, X3_AT)
-        gather_a(1, 896, 128, on_x3)
-        gather_times("b", 1, 896, 128, halves(work_v, 128), on_x3)
-        gather_times("c", 1, 896, 128, [x4[:, 2, :], x4[:, 3, :]], halves(work_v, 128))
+        gather_times("c", 1, 768, 128, [x_end[:, 0, 128:256], x_end[:, 1, 128:256]], halves(work_v, 128))
         quantize_y(0)
-        round_x(last, x4[:], LAST_AT)
+        x_grouped[last] = placed("x_grouped_last", [P, PACK * 128], BF16, LAST_AT)
+        nc.vector.tensor_copy(
+            x_grouped[last][:].rearrange("p (c i u h) -> p c u h i", i=4, u=2, h=2),
+            x_end[:, 0:2, :].rearrange("p h (u c i) -> p c u h i", u=2, i=4),
+        )
         quantize_x(last)
         multiply(last)
         finish(last)

@@ -20,22 +20,33 @@ RELU = mybir.ActivationFunctionType.Relu
 
 P = 128
 PACK = 4
-BANK = 512
-HALF = 768
-STRETCHES = ((0, 256), (256, 256), (512, 256), (896, 128), (768, 128))
+PER_COLUMN = 16
+LINE = 4
+BANKS = 8
+LONG = 256
+SHORT = 128
+EARLY = 3 * LONG
+STRETCHES = ((0, LONG), (LONG, LONG), (2 * LONG, LONG), (EARLY + SHORT, SHORT), (EARLY, SHORT))
+LAST = len(STRETCHES) - 1
+VECTOR_SHARE = 88
+X_AT = 0
+CODES_AT = X_AT + PACK * EARLY * 4
+Y_CODES_AT = CODES_AT + PACK * LONG * 2
+HELD_AT = Y_CODES_AT + (EARLY - SHORT) * 4
 
 
 def tile_attend_planefeatures_pl_kernel(tc, pa, pb, pc_, wo, bias, offs, offs2, offs3, out_0, out_1, out_2):
     nc = tc.nc
-    last = len(STRETCHES) - 1
 
     with ExitStack() as ctx:
         keep = ctx.enter_context(tc.tile_pool(name="keep", bufs=1))
         laid = ctx.enter_context(tc.tile_pool(name="laid", bufs=1))
-        psum = ctx.enter_context(tc.psum_pool(name="psum", bufs=8))
+        psum = ctx.enter_context(tc.psum_pool(name="psum", bufs=BANKS))
 
-        def placed(name, shape, dtype, offset):
-            return laid.tile(shape, dtype, name=name, offset=offset, align_bytes=64)
+        def new_tile(name, shape, dtype, at=None):
+            if at is None:
+                return keep.tile(shape, dtype, name=name, align_bytes=64)
+            return laid.tile(shape, dtype, name=name, offset=at, align_bytes=64)
 
         lists = {}
         tables = {}
@@ -47,72 +58,68 @@ def tile_attend_planefeatures_pl_kernel(tc, pa, pb, pc_, wo, bias, offs, offs2, 
                     tables[name, t] = keep.tile([P, U], F32, name="table_%s%d" % (name, t))
                     nc.sync.dma_start(tables[name, t][:], table.rearrange("(p t) u -> p t u", t=PACK)[:, t, :])
                     if t == 0:
-                        lists[name] = keep.tile([P, I // 16], U16, name="list_" + name)
+                        lists[name] = keep.tile([P, I // PER_COLUMN], U16, name="list_" + name)
                         nc.sync.dma_start(lists[name][:], offsets)
             if pair == 0:
                 w_raw = keep.tile([P, PACK * F], F32)
                 nc.sync.dma_start(w_raw[:], wo.rearrange("(p j) f -> p (j f)", j=PACK))
-        X_AT, CODES_AT, LAST_AT = 0, 12288, 16384
         bias_sb = keep.tile([P, PACK], F32)
         nc.sync.dma_start(bias_sb[:], bias.rearrange("(p t) o -> p (t o)", t=PACK))
 
-        work_u = keep.tile([P, 2 * HALF], F32)
-        work_v = keep.tile([P, 2 * HALF], F32)
+        work_u = keep.tile([P, 2 * EARLY], F32)
+        work_v = keep.tile([P, 2 * EARLY], F32)
         y_scales = keep.tile([P, I], U8, align_bytes=64)
         out_rows = out_0.rearrange("(p t) i -> p t i", t=PACK)
         out_words = out_1[0].rearrange("p c r -> p (c r)").bitcast(I32)
         out_scales = out_2[0].bitcast(I32)
 
-        def looked_up(name, t, first, n):
-            return tables[name, t][:].indirect(lists[name][:, first // 16 : (first + n) // 16])
-
         def halves(work, n):
-            return [work[:, 0:n], work[:, HALF : HALF + n]]
+            return [work[:, 0:n], work[:, EARLY : EARLY + n]]
 
-        def gather_a(pair, first, n, dst):
+        def looked_up(name, t, first, n):
+            return tables[name, t][:].indirect(lists[name][:, first // PER_COLUMN : (first + n) // PER_COLUMN])
+
+        def gather(dst, t, first, n):
+            nc.vector.tensor_copy(dst, looked_up("a", t, first, n))
+
+        def gather_times(dst, name, t, first, n, factor):
+            nc.vector.tensor_tensor(dst, looked_up(name, t, first, n), factor, MULT)
+
+        def gather_pair(dst, pair, first, n):
             for h in range(2):
-                nc.vector.tensor_copy(dst[h], looked_up("a", 2 * pair + h, first, n))
+                gather(dst[h], 2 * pair + h, first, n)
 
-        def gather_times(name, pair, first, n, dst, factor):
+        def gather_pair_times(dst, name, pair, first, n, factor):
             for h in range(2):
-                nc.vector.tensor_tensor(dst[h], looked_up(name, 2 * pair + h, first, n), factor[h], MULT)
+                gather_times(dst[h], name, 2 * pair + h, first, n, factor[h])
 
-        def interleave(grouped, planes, on_vector):
-            dst = grouped[:].rearrange("p (c i t) -> p c t i", i=4, t=PACK)
-            src = planes.rearrange("p t (c i) -> p c t i", i=4)
-            if on_vector:
-                nc.vector.tensor_copy(dst, src)
-            else:
-                nc.scalar.activation(dst, src, COPY)
+        def regroup_views(grouped, rows):
+            return (
+                grouped.rearrange("p (c i t) -> p c t i", i=LINE, t=PACK),
+                rows.rearrange("p t (c i) -> p c t i", i=LINE),
+            )
 
-        x_grouped, x_codes, x_scales, y, y_grouped, banks = {}, {}, {}, {}, {}, {}
+        x_grouped, x_codes, x_scales, y, y_grouped, z = {}, {}, {}, {}, {}, {}
 
-        def round_x(j, planes, at=None):
-            n = STRETCHES[j][1]
-            if at is None:
-                x_grouped[j] = keep.tile([P, PACK * n], BF16, name="x_grouped%d" % j, align_bytes=64)
-            else:
-                x_grouped[j] = placed("x_grouped%d" % j, [P, PACK * n], BF16, at)
-            interleave(x_grouped[j], planes, False)
+        def round_x(j, rows, at=None):
+            x_grouped[j] = new_tile("x_grouped%d" % j, [P, PACK * STRETCHES[j][1]], BF16, at)
+            nc.scalar.activation(*regroup_views(x_grouped[j][:], rows), COPY)
 
         def quantize_x(j, at=None):
             n = STRETCHES[j][1]
-            if at is None:
-                x_codes[j] = keep.tile([P, n], U32, name="x_codes%d" % j, align_bytes=64)
-            else:
-                x_codes[j] = placed("x_codes%d" % j, [P, n], U32, at)
-            x_scales[j] = keep.tile([P, n], U8, name="x_scales%d" % j, align_bytes=64)
+            x_codes[j] = new_tile("x_codes%d" % j, [P, n], U32, at)
+            x_scales[j] = new_tile("x_scales%d" % j, [P, n], U8)
             nc.vector.quantize_mx(out=x_codes[j][:].bitcast(FP8X4), scales=x_scales[j][:], in_=x_grouped[j][:])
 
         def multiply(j):
             n = STRETCHES[j][1]
-            per_bank = 1 if j == last else BANK // n
+            per_bank = n // SHORT
             for t in range(PACK):
                 if t % per_bank == 0:
                     bank = psum.tile([P, per_bank, n], F32, name="bank")
-                banks[j, t] = bank[:, t % per_bank, :]
+                z[j, t] = bank[:, t % per_bank, :]
                 nc.tensor.matmul_mx(
-                    out=banks[j, t],
+                    out=z[j, t],
                     lhsT=w_codes[:, t * P : (t + 1) * P].bitcast(FP8X4),
                     lhsT_scale=w_scales[:, t * P : (t + 1) * P],
                     rhs=x_codes[j][:].bitcast(FP8X4),
@@ -125,101 +132,114 @@ def tile_attend_planefeatures_pl_kernel(tc, pa, pb, pc_, wo, bias, offs, offs2, 
             first, n = STRETCHES[j]
             y[j] = keep.tile([P, PACK, n], F32, name="y%d" % j)
             for t in range(PACK):
-                if j == last and t % 2 == 1:
-                    nc.vector.tensor_scalar(y[j][:, t, :], banks[j, t], bias_sb[:, t : t + 1], 0.0, ADD, MAX)
+                if j == LAST and t % 2 == 1:
+                    nc.vector.tensor_scalar(y[j][:, t, :], z[j, t], bias_sb[:, t : t + 1], 0.0, ADD, MAX)
                 else:
-                    nc.scalar.activation(y[j][:, t, :], banks[j, t], RELU, bias=bias_sb[:, t : t + 1])
+                    nc.scalar.activation(y[j][:, t, :], z[j, t], RELU, bias=bias_sb[:, t : t + 1])
             nc.sync.dma_start(out_rows[:, :, first : first + n], y[j][:])
 
         def round_y(j):
-            y_grouped[j] = keep.tile([P, PACK * STRETCHES[j][1]], BF16, name="y_grouped%d" % j, align_bytes=64)
-            interleave(y_grouped[j], y[j][:], j == last)
+            y_grouped[j] = new_tile("y_grouped%d" % j, [P, PACK * STRETCHES[j][1]], BF16)
+            nc.scalar.activation(*regroup_views(y_grouped[j][:], y[j][:]), COPY)
 
-        def quantize_y(j, at=None):
+        def quantize_y(j, y_codes):
             first, n = STRETCHES[j]
-            cols = slice(first, first + n)
-            if at is None:
-                y_codes = keep.tile([P, n], U32, name="y_codes%d" % j, align_bytes=64)
-            else:
-                y_codes = placed("y_codes%d" % j, [P, n], U32, at)
-            nc.vector.quantize_mx(out=y_codes[:].bitcast(FP8X4), scales=y_scales[:, cols], in_=y_grouped[j][:])
-            nc.sync.dma_start(out_words[:, cols], y_codes[:].bitcast(I32))
+            nc.vector.quantize_mx(out=y_codes.bitcast(FP8X4), scales=y_scales[:, first : first + n], in_=y_grouped[j][:])
 
         w_grouped = keep.tile([P, PACK * F], BF16, align_bytes=64)
         w_codes = keep.tile([P, F], U32, align_bytes=64)
         w_scales = keep.tile([P, F], U8, align_bytes=64)
 
-        x = placed("x", [P, PACK, 768], F32, X_AT)
-        gather_a(0, 0, 768, halves(work_u, 768))
-        gather_times("b", 0, 0, 768, halves(work_v, 768), halves(work_u, 768))
-        gather_times("c", 0, 0, 768, [x[:, 0, :], x[:, 1, :]], halves(work_v, 768))
+        x_long = new_tile("x_long", [P, PACK, EARLY], F32, X_AT)
+        part = [slice(s * LONG, (s + 1) * LONG) for s in range(3)]
+        gather_pair(halves(work_u, EARLY), 0, 0, EARLY)
+        gather_pair_times(halves(work_v, EARLY), "b", 0, 0, EARLY, halves(work_u, EARLY))
+        gather_pair_times([x_long[:, 0, :], x_long[:, 1, :]], "c", 0, 0, EARLY, halves(work_v, EARLY))
+
         nc.scalar.activation(
             w_grouped[:].rearrange("p (t m j) -> p m j t", t=PACK, j=PACK),
             w_raw[:].rearrange("p (j m t) -> p m j t", t=PACK, j=PACK),
             COPY,
         )
-        gather_a(1, 0, 512, halves(work_v, 512))
-        nc.vector.quantize_mx(out=w_codes[:].bitcast(FP8X4), scales=w_scales[:], in_=w_grouped[:])
-        near = [work_u[:, 0:512], work_u[:, 512:1024]]
-        gather_times("b", 1, 0, 512, near, halves(work_v, 512))
-        nc.vector.tensor_tensor(x[:, 2, 0:512], looked_up("c", 2, 0, 512), near[0], MULT)
-        for first in (0, 256):
-            nc.vector.tensor_tensor(
-                x[:, 3, first : first + 256], looked_up("c", 3, first, 256), work_u[:, 512 + first : 768 + first], MULT
-            )
-        round_x(0, x[:, :, 0:256])
-        round_x(1, x[:, :, 256:512])
 
-        middle = [work_u[:, 384:640], work_u[:, 640:896]]
-        gather_a(1, 512, 256, middle)
+        gather_pair(halves(work_v, 2 * LONG), 1, 0, 2 * LONG)
+        nc.vector.quantize_mx(out=w_codes[:].bitcast(FP8X4), scales=w_scales[:], in_=w_grouped[:])
+        gather_pair_times(
+            [work_u[:, 0 : 2 * LONG], x_long[:, 2, LONG:EARLY]], "b", 1, 0, 2 * LONG, halves(work_v, 2 * LONG)
+        )
+        gather_times(x_long[:, 2, part[0]], "c", 2, 0, LONG, work_u[:, part[0]])
+        gather_times(x_long[:, 3, part[0]], "c", 3, 0, LONG, x_long[:, 2, part[1]])
+        round_x(0, x_long[:, :, part[0]])
+        gather_times(x_long[:, 3, part[1]], "c", 3, LONG, LONG, x_long[:, 2, part[2]])
+        gather_times(x_long[:, 2, part[1]], "c", 2, LONG, LONG, work_u[:, part[1]])
+        round_x(1, x_long[:, :, part[1]])
+
+        gather(x_long[:, 2, part[2]], 2, 2 * LONG, LONG)
         quantize_x(0, CODES_AT)
         multiply(0)
         finish(0)
         round_y(0)
-        freed = [x[:, 0, 0:256], x[:, 1, 0:256]]
-        gather_times("b", 1, 512, 256, freed, middle)
-        gather_times("c", 1, 512, 256, [x[:, 2, 512:768], x[:, 3, 512:768]], freed)
-        round_x(2, x[:, :, 512:768], CODES_AT)
+        gather(x_long[:, 0, part[0]], 3, 2 * LONG, LONG)
+        partial = [x_long[:, 1, part[0]], work_u[:, part[0]]]
+        gather_pair_times(partial, "b", 1, 2 * LONG, LONG, [x_long[:, 2, part[2]], x_long[:, 0, part[0]]])
+        gather_pair_times([x_long[:, 2, part[2]], x_long[:, 3, part[2]]], "c", 1, 2 * LONG, LONG, partial)
+        round_x(2, x_long[:, :, part[2]], CODES_AT)
         quantize_x(1)
         multiply(1)
         finish(1)
         round_y(1)
 
-        freed = [x[:, 0, 256:512], x[:, 1, 256:512]]
-        gather_a(0, 768, 256, freed)
-        gather_times("b", 0, 768, 256, halves(work_v, 256), freed)
+        start = [x_long[:, 0, part[1]], x_long[:, 1, part[1]]]
+        gather_pair(start, 0, EARLY, 2 * SHORT)
+        gather_pair_times(halves(work_v, 2 * SHORT), "b", 0, EARLY, 2 * SHORT, start)
         quantize_x(2)
         multiply(2)
         finish(2)
-        x_end = placed("x_end", [P, PACK, 256], F32, X_AT)
-        gather_times("c", 0, 768, 256, [x_end[:, 0, :], x_end[:, 1, :]], halves(work_v, 256))
+        x_short = new_tile("x_short", [P, PACK, 2 * SHORT], F32, X_AT)
+        upper = slice(SHORT, 2 * SHORT)
+        gather_pair_times([x_short[:, 0, :], x_short[:, 1, :]], "c", 0, EARLY, 2 * SHORT, halves(work_v, 2 * SHORT))
         round_y(2)
-        gather_a(1, 896, 128, halves(work_v, 128))
-        gather_times("b", 1, 896, 128, halves(work_u, 128), halves(work_v, 128))
-        gather_times("c", 1, 896, 128, [x_end[:, 2, 128:256], x_end[:, 3, 128:256]], halves(work_u, 128))
-        round_x(3, x_end[:, :, 128:256])
 
-        gather_a(1, 768, 128, halves(work_u, 128))
-        gather_times("b", 1, 768, 128, halves(work_v, 128), halves(work_u, 128))
+        first = STRETCHES[3][0]
+        gather_pair(halves(work_v, SHORT), 1, first, SHORT)
+        gather_pair_times(halves(work_u, SHORT), "b", 1, first, SHORT, halves(work_v, SHORT))
+        gather_pair_times([x_short[:, 2, upper], x_short[:, 3, upper]], "c", 1, first, SHORT, halves(work_u, SHORT))
+        round_x(3, x_short[:, :, upper])
+
+        first = STRETCHES[LAST][0]
+        gather_pair(halves(work_u, SHORT), 1, first, SHORT)
+        held = [new_tile("held%d" % h, [P, SHORT], F32, HELD_AT + SHORT * 4 * h)[:] for h in range(2)]
+        gather_pair_times(held, "b", 1, first, SHORT, halves(work_u, SHORT))
         quantize_x(3)
         multiply(3)
         finish(3)
         round_y(3)
-        gather_times("c", 1, 768, 128, [x_end[:, 0, 128:256], x_end[:, 1, 128:256]], halves(work_v, 128))
-        quantize_y(0)
-        x_grouped[last] = placed("x_grouped_last", [P, PACK * 128], BF16, LAST_AT)
+        gather_pair_times([x_short[:, 0, upper], x_short[:, 1, upper]], "c", 1, first, SHORT, held)
+
+        x_grouped[LAST] = new_tile("x_grouped_last", [P, PACK * SHORT], BF16)
         nc.vector.tensor_copy(
-            x_grouped[last][:].rearrange("p (c i u h) -> p c u h i", i=4, u=2, h=2),
-            x_end[:, 0:2, :].rearrange("p h (u c i) -> p c u h i", u=2, i=4),
+            x_grouped[LAST][:].rearrange("p (c i u h) -> p c u h i", i=LINE, u=2, h=2),
+            x_short[:, 0:2, :].rearrange("p h (u c i) -> p c u h i", u=2, i=LINE),
         )
-        quantize_x(last)
-        multiply(last)
-        finish(last)
-        round_y(last)
-        quantize_y(last)
-        quantize_y(1, LAST_AT - 768)
-        quantize_y(2, LAST_AT + 768)
-        quantize_y(3, LAST_AT + 256)
-        for q in range(4):
-            queue = nc.sync if q % 2 == 0 else nc.scalar
-            queue.dma_start(out_scales[4 * q : 4 * q + 4, :], y_scales[32 * q : 32 * q + 4, :].bitcast(I32))
+        quantize_x(LAST)
+        multiply(LAST)
+        finish(LAST)
+        y_grouped[LAST] = new_tile("y_grouped_last", [P, PACK * SHORT], BF16)
+        cut = PACK * VECTOR_SHARE
+        nc.vector.tensor_copy(*regroup_views(y_grouped[LAST][:, :cut], y[LAST][:, :, :VECTOR_SHARE]))
+        nc.scalar.activation(*regroup_views(y_grouped[LAST][:, cut:], y[LAST][:, :, VECTOR_SHARE:]), COPY)
+        last_codes = keep.tile([P, SHORT], U32, align_bytes=64)
+        quantize_y(LAST, last_codes[:])
+        nc.sync.dma_start(out_words[:, EARLY : EARLY + SHORT], last_codes[:].bitcast(I32))
+
+        long_codes = new_tile("long_codes", [P, EARLY], U32, Y_CODES_AT)
+        for j in range(3):
+            quantize_y(j, long_codes[:, part[j]])
+        nc.sync.dma_start(out_words[:, 0:EARLY], long_codes[:].bitcast(I32))
+        short_codes = keep.tile([P, SHORT], U32, align_bytes=64)
+        quantize_y(3, short_codes[:])
+        nc.sync.dma_start(out_words[:, EARLY + SHORT : I], short_codes[:].bitcast(I32))
+
+        for g in range(4):
+            queue = nc.sync if g % 2 == 0 else nc.scalar
+            queue.dma_start(out_scales[4 * g : 4 * g + 4, :], y_scales[32 * g : 32 * g + 4, :].bitcast(I32))

from contextlib import ExitStack

import concourse.mybir as mybir

K, U, I, F = 512, 1024, 1024, 512
FLOPS = 2 * K * F * I

F32 = mybir.dt.float32
BF16 = mybir.dt.bfloat16
I32 = mybir.dt.int32
U32 = mybir.dt.uint32
U16 = mybir.dt.uint16
U8 = mybir.dt.uint8
FP8X4 = mybir.dt.float8_e4m3fn_x4
MULT = mybir.AluOpType.mult
ADD = mybir.AluOpType.add
MAX = mybir.AluOpType.max
COPY = mybir.ActivationFunctionType.Copy
RELU = mybir.ActivationFunctionType.Relu

P = 128
PACK = 4
PER_COLUMN = 16
LINE = 4
BANKS = 8
LONG = 256
SHORT = 128
EARLY = 3 * LONG
STRETCHES = ((0, LONG), (LONG, LONG), (2 * LONG, LONG), (EARLY + SHORT, SHORT), (EARLY, SHORT))
LAST = len(STRETCHES) - 1
VECTOR_SHARE = 88
X_AT = 0
CODES_AT = X_AT + PACK * EARLY * 4
Y_CODES_AT = CODES_AT + PACK * LONG * 2
HELD_AT = Y_CODES_AT + (EARLY - SHORT) * 4


def tile_attend_planefeatures_pl_kernel(tc, pa, pb, pc_, wo, bias, offs, offs2, offs3, out_0, out_1, out_2):
    nc = tc.nc

    with ExitStack() as ctx:
        keep = ctx.enter_context(tc.tile_pool(name="keep", bufs=1))
        laid = ctx.enter_context(tc.tile_pool(name="laid", bufs=1))
        psum = ctx.enter_context(tc.psum_pool(name="psum", bufs=BANKS))

        def new_tile(name, shape, dtype, at=None):
            if at is None:
                return keep.tile(shape, dtype, name=name, align_bytes=64)
            return laid.tile(shape, dtype, name=name, offset=at, align_bytes=64)

        lists = {}
        tables = {}
        sources = {"a": (pa, offs), "b": (pb, offs2), "c": (pc_, offs3)}
        for pair in range(2):
            for name in "abc":
                table, offsets = sources[name]
                for t in (2 * pair, 2 * pair + 1):
                    tables[name, t] = keep.tile([P, U], F32, name="table_%s%d" % (name, t))
                    nc.sync.dma_start(tables[name, t][:], table.rearrange("(p t) u -> p t u", t=PACK)[:, t, :])
                    if t == 0:
                        lists[name] = keep.tile([P, I // PER_COLUMN], U16, name="list_" + name)
                        nc.sync.dma_start(lists[name][:], offsets)
            if pair == 0:
                w_raw = keep.tile([P, PACK * F], F32)
                nc.sync.dma_start(w_raw[:], wo.rearrange("(p j) f -> p (j f)", j=PACK))
        bias_sb = keep.tile([P, PACK], F32)
        nc.sync.dma_start(bias_sb[:], bias.rearrange("(p t) o -> p (t o)", t=PACK))

        work_u = keep.tile([P, 2 * EARLY], F32)
        work_v = keep.tile([P, 2 * EARLY], F32)
        y_scales = keep.tile([P, I], U8, align_bytes=64)
        out_rows = out_0.rearrange("(p t) i -> p t i", t=PACK)
        out_words = out_1[0].rearrange("p c r -> p (c r)").bitcast(I32)
        out_scales = out_2[0].bitcast(I32)

        def halves(work, n):
            return [work[:, 0:n], work[:, EARLY : EARLY + n]]

        def looked_up(name, t, first, n):
            return tables[name, t][:].indirect(lists[name][:, first // PER_COLUMN : (first + n) // PER_COLUMN])

        def gather(dst, t, first, n):
            nc.vector.tensor_copy(dst, looked_up("a", t, first, n))

        def gather_times(dst, name, t, first, n, factor):
            nc.vector.tensor_tensor(dst, looked_up(name, t, first, n), factor, MULT)

        def gather_pair(dst, pair, first, n):
            for h in range(2):
                gather(dst[h], 2 * pair + h, first, n)

        def gather_pair_times(dst, name, pair, first, n, factor):
            for h in range(2):
                gather_times(dst[h], name, 2 * pair + h, first, n, factor[h])

        def regroup_views(grouped, rows):
            return (
                grouped.rearrange("p (c i t) -> p c t i", i=LINE, t=PACK),
                rows.rearrange("p t (c i) -> p c t i", i=LINE),
            )

        x_grouped, x_codes, x_scales, y, y_grouped, z = {}, {}, {}, {}, {}, {}

        def round_x(j, rows, at=None):
            x_grouped[j] = new_tile("x_grouped%d" % j, [P, PACK * STRETCHES[j][1]], BF16, at)
            nc.scalar.activation(*regroup_views(x_grouped[j][:], rows), COPY)

        def quantize_x(j, at=None):
            n = STRETCHES[j][1]
            x_codes[j] = new_tile("x_codes%d" % j, [P, n], U32, at)
            x_scales[j] = new_tile("x_scales%d" % j, [P, n], U8)
            nc.vector.quantize_mx(out=x_codes[j][:].bitcast(FP8X4), scales=x_scales[j][:], in_=x_grouped[j][:])

        def multiply(j):
            n = STRETCHES[j][1]
            per_bank = n // SHORT
            for t in range(PACK):
                if t % per_bank == 0:
                    bank = psum.tile([P, per_bank, n], F32, name="bank")
                z[j, t] = bank[:, t % per_bank, :]
                nc.tensor.matmul_mx(
                    out=z[j, t],
                    lhsT=w_codes[:, t * P : (t + 1) * P].bitcast(FP8X4),
                    lhsT_scale=w_scales[:, t * P : (t + 1) * P],
                    rhs=x_codes[j][:].bitcast(FP8X4),
                    rhs_scale=x_scales[j][:],
                    start=True,
                    stop=True,
                )

        def finish(j):
            first, n = STRETCHES[j]
            y[j] = keep.tile([P, PACK, n], F32, name="y%d" % j)
            for t in range(PACK):
                if j == LAST and t % 2 == 1:
                    nc.vector.tensor_scalar(y[j][:, t, :], z[j, t], bias_sb[:, t : t + 1], 0.0, ADD, MAX)
                else:
                    nc.scalar.activation(y[j][:, t, :], z[j, t], RELU, bias=bias_sb[:, t : t + 1])
            nc.sync.dma_start(out_rows[:, :, first : first + n], y[j][:])

        def round_y(j):
            y_grouped[j] = new_tile("y_grouped%d" % j, [P, PACK * STRETCHES[j][1]], BF16)
            nc.scalar.activation(*regroup_views(y_grouped[j][:], y[j][:]), COPY)

        def quantize_y(j, y_codes):
            first, n = STRETCHES[j]
            nc.vector.quantize_mx(out=y_codes.bitcast(FP8X4), scales=y_scales[:, first : first + n], in_=y_grouped[j][:])

        w_grouped = keep.tile([P, PACK * F], BF16, align_bytes=64)
        w_codes = keep.tile([P, F], U32, align_bytes=64)
        w_scales = keep.tile([P, F], U8, align_bytes=64)

        x_long = new_tile("x_long", [P, PACK, EARLY], F32, X_AT)
        part = [slice(s * LONG, (s + 1) * LONG) for s in range(3)]
        gather_pair(halves(work_u, EARLY), 0, 0, EARLY)
        gather_pair_times(halves(work_v, EARLY), "b", 0, 0, EARLY, halves(work_u, EARLY))
        gather_pair_times([x_long[:, 0, :], x_long[:, 1, :]], "c", 0, 0, EARLY, halves(work_v, EARLY))

        nc.scalar.activation(
            w_grouped[:].rearrange("p (t m j) -> p m j t", t=PACK, j=PACK),
            w_raw[:].rearrange("p (j m t) -> p m j t", t=PACK, j=PACK),
            COPY,
        )

        gather_pair(halves(work_v, 2 * LONG), 1, 0, 2 * LONG)
        nc.vector.quantize_mx(out=w_codes[:].bitcast(FP8X4), scales=w_scales[:], in_=w_grouped[:])
        gather_pair_times(
            [work_u[:, 0 : 2 * LONG], x_long[:, 2, LONG:EARLY]], "b", 1, 0, 2 * LONG, halves(work_v, 2 * LONG)
        )
        gather_times(x_long[:, 2, part[0]], "c", 2, 0, LONG, work_u[:, part[0]])
        gather_times(x_long[:, 3, part[0]], "c", 3, 0, LONG, x_long[:, 2, part[1]])
        round_x(0, x_long[:, :, part[0]])
        gather_times(x_long[:, 3, part[1]], "c", 3, LONG, LONG, x_long[:, 2, part[2]])
        gather_times(x_long[:, 2, part[1]], "c", 2, LONG, LONG, work_u[:, part[1]])
        round_x(1, x_long[:, :, part[1]])

        gather(x_long[:, 2, part[2]], 2, 2 * LONG, LONG)
        quantize_x(0, CODES_AT)
        multiply(0)
        finish(0)
        round_y(0)
        gather(x_long[:, 0, part[0]], 3, 2 * LONG, LONG)
        partial = [x_long[:, 1, part[0]], work_u[:, part[0]]]
        gather_pair_times(partial, "b", 1, 2 * LONG, LONG, [x_long[:, 2, part[2]], x_long[:, 0, part[0]]])
        gather_pair_times([x_long[:, 2, part[2]], x_long[:, 3, part[2]]], "c", 1, 2 * LONG, LONG, partial)
        round_x(2, x_long[:, :, part[2]], CODES_AT)
        quantize_x(1)
        multiply(1)
        finish(1)
        round_y(1)

        start = [x_long[:, 0, part[1]], x_long[:, 1, part[1]]]
        gather_pair(start, 0, EARLY, 2 * SHORT)
        gather_pair_times(halves(work_v, 2 * SHORT), "b", 0, EARLY, 2 * SHORT, start)
        quantize_x(2)
        multiply(2)
        finish(2)
        x_short = new_tile("x_short", [P, PACK, 2 * SHORT], F32, X_AT)
        upper = slice(SHORT, 2 * SHORT)
        gather_pair_times([x_short[:, 0, :], x_short[:, 1, :]], "c", 0, EARLY, 2 * SHORT, halves(work_v, 2 * SHORT))
        round_y(2)

        first = STRETCHES[3][0]
        gather_pair(halves(work_v, SHORT), 1, first, SHORT)
        gather_pair_times(halves(work_u, SHORT), "b", 1, first, SHORT, halves(work_v, SHORT))
        gather_pair_times([x_short[:, 2, upper], x_short[:, 3, upper]], "c", 1, first, SHORT, halves(work_u, SHORT))
        round_x(3, x_short[:, :, upper])

        first = STRETCHES[LAST][0]
        gather_pair(halves(work_u, SHORT), 1, first, SHORT)
        held = [new_tile("held%d" % h, [P, SHORT], F32, HELD_AT + SHORT * 4 * h)[:] for h in range(2)]
        gather_pair_times(held, "b", 1, first, SHORT, halves(work_u, SHORT))
        quantize_x(3)
        multiply(3)
        finish(3)
        round_y(3)
        gather_pair_times([x_short[:, 0, upper], x_short[:, 1, upper]], "c", 1, first, SHORT, held)

        x_grouped[LAST] = new_tile("x_grouped_last", [P, PACK * SHORT], BF16)
        nc.vector.tensor_copy(
            x_grouped[LAST][:].rearrange("p (c i u h) -> p c u h i", i=LINE, u=2, h=2),
            x_short[:, 0:2, :].rearrange("p h (u c i) -> p c u h i", u=2, i=LINE),
        )
        quantize_x(LAST)
        multiply(LAST)
        finish(LAST)
        y_grouped[LAST] = new_tile("y_grouped_last", [P, PACK * SHORT], BF16)
        cut = PACK * VECTOR_SHARE
        nc.vector.tensor_copy(*regroup_views(y_grouped[LAST][:, :cut], y[LAST][:, :, :VECTOR_SHARE]))
        nc.scalar.activation(*regroup_views(y_grouped[LAST][:, cut:], y[LAST][:, :, VECTOR_SHARE:]), COPY)
        last_codes = keep.tile([P, SHORT], U32, align_bytes=64)
        quantize_y(LAST, last_codes[:])
        nc.sync.dma_start(out_words[:, EARLY : EARLY + SHORT], last_codes[:].bitcast(I32))

        long_codes = new_tile("long_codes", [P, EARLY], U32, Y_CODES_AT)
        for j in range(3):
            quantize_y(j, long_codes[:, part[j]])
        nc.sync.dma_start(out_words[:, 0:EARLY], long_codes[:].bitcast(I32))
        short_codes = keep.tile([P, SHORT], U32, align_bytes=64)
        quantize_y(3, short_codes[:])
        nc.sync.dma_start(out_words[:, EARLY + SHORT : I], short_codes[:].bitcast(I32))

        for g in range(4):
            queue = nc.sync if g % 2 == 0 else nc.scalar
            queue.dma_start(out_scales[4 * g : 4 * g + 4, :], y_scales[32 * g : 32 * g + 4, :].bitcast(I32))
